import numpy as np
import ml_dtypes


def mxq(x, axis, fmt="e4m3"):
    dtype, down = {"e4m3": (ml_dtypes.float8_e4m3fn, 7), "e5m2": (ml_dtypes.float8_e5m2, 14)}[fmt]
    v = np.moveaxis(np.asarray(x, np.float32).astype(ml_dtypes.bfloat16).astype(np.float64), axis, -1)
    blocks = v.reshape(v.shape[:-1] + (-1, 32))
    amax = np.abs(blocks).max(-1, keepdims=True)
    byte = np.maximum(np.where(amax > 0, np.frexp(amax)[1] - 1 + 127, 0) - down, 1)
    scale = np.exp2(byte - 127.0)
    codes = (blocks / scale).astype(np.float32).astype(dtype).astype(np.float64)
    return np.moveaxis((codes * scale).reshape(v.shape), -1, axis)


WIDE = False


def mx_kscale(k):
    if not WIDE:
        return np.ones(k)
    levels = np.array([10, -10, 5, -5, 0])
    if k % 512:
        return np.exp2(np.random.permutation(np.resize(levels, k // 32))).repeat(32)
    a = np.empty((k // 512, 16))
    for p in range(k // 512):
        a[p, :8] = np.random.permutation(np.resize(levels, 8))
        for g in range(8):
            far = levels[np.abs(levels - a[p, g]) >= 10]
            a[p, g + 8] = far[np.random.randint(len(far))]
    return np.exp2(a.ravel()).repeat(32)


def f64(x):
    return np.asarray(x).astype(np.float64)


def striped(idx):
    return np.tile(idx.reshape(-1, 16).T, (8, 1)).astype(np.uint16)


def unstriped(offs):
    return offs[:16].T.reshape(-1).astype(np.int64)


E2M1 = np.array([0.0, 0.5, 1.0, 1.5, 2.0, 3.0, 4.0, 6.0, -0.0, -0.5, -1.0, -1.5, -2.0, -3.0, -4.0, -6.0])


def pack_weight(w, fmt):
    k, n = w.shape
    w = f64(np.asarray(w, np.float32).astype(ml_dtypes.bfloat16)).reshape(k // 32, 32, n)
    amax = np.abs(w).max(1)
    if fmt == "e4m3":
        byte = np.frexp(amax)[1] - 1 + 127 - 7
    else:
        mant, ex = np.frexp(amax / 6.0)
        byte = np.where(mant > 0.5, ex, ex - 1) + 127
    byte = np.clip(np.where(amax > 0, byte, 1), 1, 254)
    scaled = (w * np.exp2(127.0 - byte)[:, None, :]).reshape(k, n).astype(np.float32)
    by_word = np.ascontiguousarray(scaled.reshape(k // 512, 128, 4, n).transpose(0, 1, 3, 2))
    if fmt == "e4m3":
        words = by_word.astype(ml_dtypes.float8_e4m3fn).view(np.uint8)
    else:
        c = by_word.astype(ml_dtypes.float4_e2m1fn).view(np.uint8) & 0xF
        words = (c[..., 0::2] | (c[..., 1::2] << 4)).reshape(k // 512, 128, 2 * n)
    return np.ascontiguousarray(words), np.ascontiguousarray(byte.astype(np.uint8).reshape(k // 512, 16, n))


def unpack_weight(words, scales, fmt):
    g, _, n = scales.shape
    words = np.ascontiguousarray(words).reshape(g, 128, n, -1)
    if fmt == "e4m3":
        vals = words.view(ml_dtypes.float8_e4m3fn).astype(np.float64)
    else:
        nib = np.empty((g, 128, n, 4), np.uint8)
        nib[..., 0::2] = words & 0xF
        nib[..., 1::2] = words >> 4
        vals = E2M1[nib]
    vals = vals * np.repeat(np.exp2(scales.astype(np.float64) - 127.0), 8, axis=1)[..., None]
    return vals.transpose(0, 1, 3, 2).reshape(g * 512, n)


G, K, M, T, S = 4, 1024, 128, 2048, 256


def setup_inputs():
    n = np.random.standard_normal
    s = mx_kscale(K)[:, None]
    p_w4 = pack_weight(n((K, M)) / np.sqrt(K) / s, "e2m1")
    p_w8 = pack_weight(n((K, M)) / np.sqrt(K) / s, "e4m3")
    return {
        "xT": (n((K, T)) * s).astype(np.float32),
        "c": (n((K, S)) * s).astype(np.float32),
        "w4_words": p_w4[0],
        "w4_scales": p_w4[1],
        "w8_words": p_w8[0],
        "w8_scales": p_w8[1],
        "r": (n((256, 128))).astype(np.float32),
        "offs": striped(np.concatenate([np.random.permutation(T)[:S] for _ in range(G)])),
    }


def reference(xT, c, w4_words, w4_scales, w8_words, w8_scales, r, offs):
    idx = unstriped(offs).reshape(G, S)
    d_ = [mxq(f64(xT)[:, idx[g]] - f64(c), 0, "e4m3") for g in range(G)]
    c_ = mxq(f64(c), 0, "e4m3")
    w4_ = unpack_weight(w4_words, w4_scales, "e2m1")
    w8_ = unpack_weight(w8_words, w8_scales, "e4m3")
    y = np.max([(d.T @ w4_) for d in d_], axis=0) + (c_.T @ w8_)
    return f64(r) + y

@@ -1,0 +1,147 @@
+from contextlib import ExitStack
+
+import concourse.mybir as mybir
+
+G, K, M, T, S = 4, 1024, 128, 2048, 256
+FLOPS = 2 * K * M * S * (G + 1)
+
+F32 = mybir.dt.float32
+BF16 = mybir.dt.bfloat16
+I32 = mybir.dt.int32
+U32 = mybir.dt.uint32
+U16 = mybir.dt.uint16
+U8 = mybir.dt.uint8
+FP8X4 = mybir.dt.float8_e4m3fn_x4
+FP4X4 = mybir.dt.float4_e2m1fn_x4
+ALU = mybir.AluOpType
+
+P = 128
+PACK = 4
+PASSES = K // (P * PACK)
+HALVES = S // P
+
+
+def tile_list_edge_tm_res_kernel(tc, xT, c, w4_words, w4_scales, w8_words, w8_scales, r, offs, out):
+    nc = tc.nc
+    with ExitStack() as ctx:
+        keep = ctx.enter_context(tc.tile_pool(name="keep", bufs=1))
+        ring = ctx.enter_context(tc.tile_pool(name="ring", bufs=3))
+        psum = ctx.enter_context(tc.psum_pool(name="psum", bufs=1))
+
+        offsets = keep.tile([P, G * S // 16], U16, name="offsets")
+        nc.sync.dma_start(offsets[:], offs)
+
+        w4_sc = keep.tile([P, PASSES, M], U8, name="w4_sc", align_bytes=64)
+        w8_sc = keep.tile([P, PASSES, M], U8, name="w8_sc", align_bytes=64)
+        nc.vector.memset(w4_sc[:].bitcast(I32), 0)
+        nc.vector.memset(w8_sc[:].bitcast(I32), 0)
+
+        x_rows = xT.rearrange("(a p i) t -> a i p t", a=PASSES, i=PACK)
+        c_rows = c.rearrange("(a p i) j -> a p i j", a=PASSES, i=PACK)
+        x_sb = [[keep.tile([P, T], F32, name="x_%d_%d" % (a, i)) for i in range(PACK)] for a in range(PASSES)]
+        c_sb = [keep.tile([P, PACK, S], F32, name="c_%d" % a) for a in range(PASSES)]
+        nc.sync.dma_start(c_sb[0][:, 0:1, :], c_rows[0][:, 0:1, :])
+        nc.sync.dma_start(x_sb[0][0][:], x_rows[0][0])
+        nc.sync.dma_start(c_sb[0][:, 1:PACK, :], c_rows[0][:, 1:PACK, :])
+        for i in range(1, PACK):
+            nc.sync.dma_start(x_sb[0][i][:], x_rows[0][i])
+        nc.sync.dma_start(c_sb[1][:], c_rows[1])
+        for i in range(PACK):
+            nc.sync.dma_start(x_sb[1][i][:], x_rows[1][i])
+
+        w4_sb = keep.tile([P, PASSES, 2 * M], U8, name="w4_sb", align_bytes=64)
+        w8_sb = keep.tile([P, PASSES, 4 * M], U8, name="w8_sb", align_bytes=64)
+        r_sb = keep.tile([P, HALVES, M], F32, name="r_sb")
+        nc.sync.dma_start(w8_sb[:].bitcast(I32), w8_words.rearrange("a p n i -> p a (n i)").bitcast(I32))
+        nc.sync.dma_start(w4_sb[:].bitcast(I32), w4_words.rearrange("a p b -> p a b").bitcast(I32))
+        nc.sync.dma_start(r_sb[:], r.rearrange("(h p) n -> p h n", p=P))
+        for plane, src in ((w8_sc, w8_scales), (w4_sc, w4_scales)):
+            for q in range(4):
+                nc.sync.dma_start(plane[32 * q : 32 * q + 4, :, :].bitcast(I32),
+                                  src[:, 4 * q : 4 * q + 4, :].rearrange("a r n -> r a n").bitcast(I32))
+
+        def interleave(planes, width, name):
+            grouped = keep.tile([P, width, PACK], BF16, name="bf_" + name, align_bytes=64)
+            nc.scalar.copy(grouped[:].rearrange("p (b e) i -> p b i e", e=4),
+                           planes.rearrange("p i (b e) -> p b i e", e=4))
+            return grouped
+
+        def quantise(grouped, width, name):
+            codes = keep.tile([P, width], U32, name="codes_" + name, align_bytes=64)
+            scales = keep.tile([P, width], U8, name="scales_" + name, align_bytes=64)
+            nc.vector.quantize_mx(out=codes[:].bitcast(FP8X4), scales=scales[:],
+                                  in_=grouped[:].rearrange("p j i -> p (j i)"))
+            return codes, scales
+
+        def gather(diff, a, i, g, j0, width):
+            col = (g * S + j0) // 16
+            nc.vector.tensor_tensor(diff[:, i, :], x_sb[a][i][:].indirect(offsets[:, col : col + width // 16]),
+                                    c_sb[a][:, i, j0 : j0 + width], ALU.subtract)
+
+        def product(acc, a, operand, j0, w_sb, w_dtype, w_sc):
+            codes, scales = operand
+            nc.tensor.matmul_mx(out=acc, lhsT=codes[:, j0 : j0 + P].bitcast(FP8X4), lhsT_scale=scales[:, j0 : j0 + P],
+                                rhs=w_sb[:, a, :].bitcast(w_dtype), rhs_scale=w_sc[:, a, :],
+                                start=(a == 0), stop=(a == PASSES - 1))
+
+        diff0 = [keep.tile([P, PACK, S], F32, name="diff0_%d" % g) for g in range(G)]
+        c_q = [None, None]
+        d0_q = []
+        for i in range(PACK):
+            for g in range(G):
+                gather(diff0[g], 0, i, g, 0, S)
+            if i == 1:
+                c_q[0] = quantise(interleave(c_sb[0][:], S, "c0"), S, "c0")
+        d0_bf = [interleave(diff0[g][:], S, "d0_%d" % g) for g in range(G)]
+        c1_bf = interleave(c_sb[1][:], S, "c1")
+
+        diff1 = [ring.tile([P, PACK, S], F32, name="diff1", tag="diff1") for g in range(G - 1)]
+        for i in range(PACK):
+            for g in range(G - 1):
+                gather(diff1[g], 1, i, g, 0, S)
+            if i == 0:
+                d0_q = [quantise(d0_bf[g], S, "d0_%d" % g) for g in range(G)]
+            if i == 1:
+                c_q[1] = quantise(c1_bf, S, "c1")
+        d1_bf = [interleave(diff1[g][:], S, "d1_%d" % g) for g in range(G - 1)]
+        last = ring.tile([P, HALVES, PACK, P], F32, name="diff1", tag="diff1")
+        last_bf = []
+        for h in range(HALVES):
+            for i in range(PACK):
+                gather(last[:, h], 1, i, G - 1, h * P, P)
+            last_bf.append(interleave(last[:, h], P, "last_%d" % h))
+
+        own = psum.tile([P, HALVES, M], F32, name="own")
+        for h in range(HALVES):
+            for a in range(PASSES):
+                product(own[:, h, :], a, c_q[a], h * P, w8_sb, FP8X4, w8_sc)
+        base = keep.tile([P, HALVES, M], F32, name="base")
+        nc.vector.tensor_tensor(base[:], own[:], r_sb[:], ALU.add)
+
+        edge_last = [psum.tile([P, M], F32, name="edge_last_%d" % h) for h in range(HALVES)]
+        for h in range(HALVES):
+            product(edge_last[h][:], 0, d0_q[G - 1], h * P, w4_sb, FP4X4, w4_sc)
+
+        best = None
+        for g in range(G - 1):
+            d1_q = quantise(d1_bf[g], S, "d1_%d" % g)
+            edge = psum.tile([P, HALVES, M], F32, name="edge_%d" % g)
+            for h in range(HALVES):
+                product(edge[:, h, :], 0, d0_q[g], h * P, w4_sb, FP4X4, w4_sc)
+                product(edge[:, h, :], 1, d1_q, h * P, w4_sb, FP4X4, w4_sc)
+            running = keep.tile([P, HALVES, M], F32, name="best_%d" % g)
+            if g == 0:
+                nc.scalar.copy(running[:], edge[:])
+            else:
+                nc.vector.tensor_tensor(running[:], edge[:], best[:], ALU.max)
+            best = running
+
+        out_rows = out.rearrange("(h p) n -> h p n", p=P)
+        for h in range(HALVES):
+            product(edge_last[h][:], 1, quantise(last_bf[h], P, "last_%d" % h), 0, w4_sb, FP4X4, w4_sc)
+        for h in range(HALVES):
+            top = keep.tile([P, M], F32, name="top_%d" % h)
+            nc.vector.tensor_tensor(top[:], edge_last[h][:], best[:, h, :], ALU.max)
+            result = keep.tile([P, M], F32, name="result_%d" % h)
+            nc.vector.tensor_tensor(result[:], top[:], base[:, h, :], ALU.add)
+            nc.sync.dma_start(out_rows[h], result[:])

@@ -1,6 +1,7 @@
 from contextlib import ExitStack
 
 import concourse.mybir as mybir
+from concourse.masks import make_identity
 
 G, K, M, T, S = 4, 1024, 128, 2048, 256
 FLOPS = 2 * K * M * S * (G + 1)
@@ -33,115 +34,135 @@ def tile_list_edge_tm_res_kernel(tc, xT, c, w4_words, w4_scales, w8_words, w8_sc
 
         w4_sc = keep.tile([P, PASSES, M], U8, name="w4_sc", align_bytes=64)
         w8_sc = keep.tile([P, PASSES, M], U8, name="w8_sc", align_bytes=64)
-        nc.vector.memset(w4_sc[:].bitcast(I32), 0)
-        nc.vector.memset(w8_sc[:].bitcast(I32), 0)
+        for plane, src in ((w4_sc, w4_scales), (w8_sc, w8_scales)):
+            nc.gpsimd.memset(plane[:].bitcast(I32), 0)
+            for q in range(4):
+                nc.gpsimd.dma_start(plane[32 * q : 32 * q + 4, :, :].bitcast(I32),
+                                    src[:, 4 * q : 4 * q + 4, :].rearrange("a r n -> r a n").bitcast(I32))
+
+        ident = keep.tile([P, P], F32, name="ident")
+        make_identity(nc, ident[:])
 
         x_rows = xT.rearrange("(a p i) t -> a i p t", a=PASSES, i=PACK)
         c_rows = c.rearrange("(a p i) j -> a p i j", a=PASSES, i=PACK)
-        x_sb = [[keep.tile([P, T], F32, name="x_%d_%d" % (a, i)) for i in range(PACK)] for a in range(PASSES)]
-        c_sb = [keep.tile([P, PACK, S], F32, name="c_%d" % a) for a in range(PASSES)]
-        nc.sync.dma_start(c_sb[0][:, 0:1, :], c_rows[0][:, 0:1, :])
-        nc.sync.dma_start(x_sb[0][0][:], x_rows[0][0])
-        nc.sync.dma_start(c_sb[0][:, 1:PACK, :], c_rows[0][:, 1:PACK, :])
-        for i in range(1, PACK):
-            nc.sync.dma_start(x_sb[0][i][:], x_rows[0][i])
-        nc.sync.dma_start(c_sb[1][:], c_rows[1])
-        for i in range(PACK):
-            nc.sync.dma_start(x_sb[1][i][:], x_rows[1][i])
-
-        w4_sb = keep.tile([P, PASSES, 2 * M], U8, name="w4_sb", align_bytes=64)
+        x_sb = [[keep.tile([P, T], F32, name="x_%d_%d" % (a, i), align_bytes=64) for i in range(PACK)] for a in range(PASSES)]
+        c_sb = [keep.tile([P, PACK, G, S], F32, name="c_%d" % a) for a in range(PASSES)]
+        c_ahead = {(0, 0): [(0, 0, 1)], (0, 1): [(0, 1, 4)], (0, 3): [(1, 0, 2)], (1, 1): [(1, 2, 4)]}
         w8_sb = keep.tile([P, PASSES, 4 * M], U8, name="w8_sb", align_bytes=64)
         r_sb = keep.tile([P, HALVES, M], F32, name="r_sb")
-        nc.sync.dma_start(w8_sb[:].bitcast(I32), w8_words.rearrange("a p n i -> p a (n i)").bitcast(I32))
+        for a in range(PASSES):
+            for i in range(PACK):
+                if (a, i) == (1, 2):
+                    nc.sync.dma_start(r_sb[:], r.rearrange("(h p) n -> p h n", p=P))
+                    nc.sync.dma_start(w8_sb[:].bitcast(I32), w8_words.rearrange("a p n i -> p a (n i)").bitcast(I32))
+                for ca, i0, i1 in c_ahead.get((a, i), []):
+                    nc.sync.dma_start(c_sb[ca][:, i0:i1, 0, :], c_rows[ca][:, i0:i1, :])
+                nc.sync.dma_start(x_sb[a][i][:], x_rows[a][i])
+
+        w4_sb = keep.tile([P, PASSES, 2 * M], U8, name="w4_sb", align_bytes=64)
         nc.sync.dma_start(w4_sb[:].bitcast(I32), w4_words.rearrange("a p b -> p a b").bitcast(I32))
-        nc.sync.dma_start(r_sb[:], r.rearrange("(h p) n -> p h n", p=P))
-        for plane, src in ((w8_sc, w8_scales), (w4_sc, w4_scales)):
-            for q in range(4):
-                nc.sync.dma_start(plane[32 * q : 32 * q + 4, :, :].bitcast(I32),
-                                  src[:, 4 * q : 4 * q + 4, :].rearrange("a r n -> r a n").bitcast(I32))
 
-        def interleave(planes, width, name):
-            grouped = keep.tile([P, width, PACK], BF16, name="bf_" + name, align_bytes=64)
-            nc.scalar.copy(grouped[:].rearrange("p (b e) i -> p b i e", e=4),
-                           planes.rearrange("p i (b e) -> p b i e", e=4))
-            return grouped
+        def interleave(grouped, planes, i0):
+            count = planes.shape[1]
+            if count == PACK:
+                nc.scalar.copy(grouped.rearrange("p (b e) i -> p b i e", e=4),
+                               planes.rearrange("p i (b e) -> p b i e", e=4))
+            else:
+                nc.scalar.copy(grouped[:, :, i0 : i0 + count], planes.rearrange("p i j -> p j i"))
 
-        def quantise(grouped, width, name):
-            codes = keep.tile([P, width], U32, name="codes_" + name, align_bytes=64)
+        def quantise(grouped, name, tag=None):
+            width = grouped.shape[1]
+            codes = keep.tile([P, width], U32, name="codes_" + name, tag=tag or "codes_" + name, align_bytes=64)
             scales = keep.tile([P, width], U8, name="scales_" + name, align_bytes=64)
             nc.vector.quantize_mx(out=codes[:].bitcast(FP8X4), scales=scales[:],
-                                  in_=grouped[:].rearrange("p j i -> p (j i)"))
+                                  in_=grouped.rearrange("p j i -> p (j i)"))
             return codes, scales
 
-        def gather(diff, a, i, g, j0, width):
-            col = (g * S + j0) // 16
-            nc.vector.tensor_tensor(diff[:, i, :], x_sb[a][i][:].indirect(offsets[:, col : col + width // 16]),
-                                    c_sb[a][:, i, j0 : j0 + width], ALU.subtract)
-
-        def product(acc, a, operand, j0, w_sb, w_dtype, w_sc):
+        def product(acc, a, operand, j0, w_sb, w_dtype, w_sc, start, stop):
             codes, scales = operand
             nc.tensor.matmul_mx(out=acc, lhsT=codes[:, j0 : j0 + P].bitcast(FP8X4), lhsT_scale=scales[:, j0 : j0 + P],
-                                rhs=w_sb[:, a, :].bitcast(w_dtype), rhs_scale=w_sc[:, a, :],
-                                start=(a == 0), stop=(a == PASSES - 1))
+                                rhs=w_sb[:, a, :].bitcast(w_dtype), rhs_scale=w_sc[:, a, :], start=start, stop=stop)
 
-        diff0 = [keep.tile([P, PACK, S], F32, name="diff0_%d" % g) for g in range(G)]
-        c_q = [None, None]
-        d0_q = []
-        for i in range(PACK):
-            for g in range(G):
-                gather(diff0[g], 0, i, g, 0, S)
-            if i == 1:
-                c_q[0] = quantise(interleave(c_sb[0][:], S, "c0"), S, "c0")
-        d0_bf = [interleave(diff0[g][:], S, "d0_%d" % g) for g in range(G)]
-        c1_bf = interleave(c_sb[1][:], S, "c1")
+        early = [psum.tile([P, G - 1, M], F32, name="early_%d" % h) for h in range(HALVES)]
+        late = [psum.tile([P, M], F32, name="late_%d" % h) for h in range(HALVES)]
 
-        diff1 = [ring.tile([P, PACK, S], F32, name="diff1", tag="diff1") for g in range(G - 1)]
-        for i in range(PACK):
-            for g in range(G - 1):
-                gather(diff1[g], 1, i, g, 0, S)
-            if i == 0:
-                d0_q = [quantise(d0_bf[g], S, "d0_%d" % g) for g in range(G)]
-            if i == 1:
-                c_q[1] = quantise(c1_bf, S, "c1")
-        d1_bf = [interleave(diff1[g][:], S, "d1_%d" % g) for g in range(G - 1)]
-        last = ring.tile([P, HALVES, PACK, P], F32, name="diff1", tag="diff1")
-        last_bf = []
-        for h in range(HALVES):
-            for i in range(PACK):
-                gather(last[:, h], 1, i, G - 1, h * P, P)
-            last_bf.append(interleave(last[:, h], P, "last_%d" % h))
-
-        own = psum.tile([P, HALVES, M], F32, name="own")
-        for h in range(HALVES):
-            for a in range(PASSES):
-                product(own[:, h, :], a, c_q[a], h * P, w8_sb, FP8X4, w8_sc)
-        base = keep.tile([P, HALVES, M], F32, name="base")
-        nc.vector.tensor_tensor(base[:], own[:], r_sb[:], ALU.add)
-
-        edge_last = [psum.tile([P, M], F32, name="edge_last_%d" % h) for h in range(HALVES)]
-        for h in range(HALVES):
-            product(edge_last[h][:], 0, d0_q[G - 1], h * P, w4_sb, FP4X4, w4_sc)
-
-        best = None
-        for g in range(G - 1):
-            d1_q = quantise(d1_bf[g], S, "d1_%d" % g)
-            edge = psum.tile([P, HALVES, M], F32, name="edge_%d" % g)
+        def edge_product(g, a, operand, j0):
             for h in range(HALVES):
-                product(edge[:, h, :], 0, d0_q[g], h * P, w4_sb, FP4X4, w4_sc)
-                product(edge[:, h, :], 1, d1_q, h * P, w4_sb, FP4X4, w4_sc)
-            running = keep.tile([P, HALVES, M], F32, name="best_%d" % g)
-            if g == 0:
-                nc.scalar.copy(running[:], edge[:])
-            else:
-                nc.vector.tensor_tensor(running[:], edge[:], best[:], ALU.max)
-            best = running
+                if g < G - 1:
+                    product(early[h][:, g, :], a, operand, j0 + h * P, w4_sb, FP4X4, w4_sc,
+                            start=(a == 0 and g == 0), stop=(a == PASSES - 1 and g == G - 2))
+                else:
+                    product(late[h][:], a, operand, j0 + h * P, w4_sb, FP4X4, w4_sc,
+                            start=(a == 0), stop=(a == PASSES - 1))
 
-        out_rows = out.rearrange("(h p) n -> h p n", p=P)
+        def wide_pair(a, i0, targets):
+            diff = keep.tile([P, 2, G, S], F32, name="diff_%d_%d" % (a, i0))
+            for e in range(2):
+                nc.vector.tensor_tensor(diff[:, e].rearrange("p g j -> p (g j)"), x_sb[a][i0 + e][:].indirect(offsets[:]),
+                                        c_sb[a][:, i0 + e].rearrange("p g j -> p (g j)"), ALU.subtract)
+            for g in range(G):
+                interleave(targets[g], diff[:, :, g, :], i0)
+
+        for a, planes in ((0, PACK), (1, 2)):
+            for i in range(planes):
+                nc.scalar.copy(c_sb[a][:, i, 1:G, :], c_sb[a][:, i, 0:1, :].to_broadcast([P, G - 1, S]))
+        c_bf = [keep.tile([P, S, PACK], BF16, name="c_bf_%d" % a, align_bytes=64) for a in range(PASSES)]
+        for a in range(PASSES):
+            interleave(c_bf[a][:], c_sb[a][:, :, 0, :], 0)
+
+        d0_bf = [keep.tile([P, 2 * S, PACK], BF16, name="d0_bf_%d" % gp, align_bytes=64) for gp in range(2)]
+        d1_bf = [keep.tile([P, S, PACK], BF16, name="d1_bf_%d" % g, align_bytes=64) for g in range(G)]
+        d0_of = [d0_bf[g // 2][:, (g % 2) * S : (g % 2 + 1) * S, :] for g in range(G)]
+        wide_pair(0, 0, d0_of)
+        wide_pair(0, 2, d0_of)
+        wide_pair(1, 0, [tile[:] for tile in d1_bf])
+        c_q = [quantise(c_bf[0][:], "c_0")]
+        for gp in range(2):
+            d0_q = quantise(d0_bf[gp][:], "d0_%d" % gp, tag="x_1_%d" % gp)
+            for gg in range(2):
+                edge_product(2 * gp + gg, 0, d0_q, gg * S)
+
+        for g in range(G):
+            width = S if g < G - 1 else P
+            diff = ring.tile([P, S // width, 2, width], F32, name="diff_last", tag="diff_last")
+            for piece in range(S // width):
+                j0 = piece * width
+                first = (g * S + j0) // 16
+                for e in range(2):
+                    nc.vector.tensor_tensor(diff[:, piece, e, :],
+                                            x_sb[1][2 + e][:].indirect(offsets[:, first : first + width // 16]),
+                                            c_sb[1][:, 2 + e, 0, j0 : j0 + width], ALU.subtract)
+                interleave(d1_bf[g][:, j0 : j0 + width, :], diff[:, piece], 2)
+        c_q.append(quantise(c_bf[1][:], "c_1", tag="d0_bf_1"))
+        r_turned = psum.tile([P, S], F32, name="r_turned")
         for h in range(HALVES):
-            product(edge_last[h][:], 1, quantise(last_bf[h], P, "last_%d" % h), 0, w4_sb, FP4X4, w4_sc)
+            nc.tensor.transpose(r_turned[:, h * P : (h + 1) * P], r_sb[:, h, :], ident[:])
+        r_t = keep.tile([P, S], F32, name="r_t")
+        nc.scalar.copy(r_t[:], r_turned[:])
+        own = psum.tile([P, S], F32, name="own")
+        for a in range(PASSES):
+            nc.tensor.matmul_mx(out=own[:], lhsT=w8_sb[:, a, :].bitcast(FP8X4), lhsT_scale=w8_sc[:, a, :],
+                                rhs=c_q[a][0][:].bitcast(FP8X4), rhs_scale=c_q[a][1][:],
+                                start=(a == 0), stop=(a == PASSES - 1))
+        own_t = keep.tile([P, S], F32, name="own_t")
+        nc.scalar.copy(own_t[:], own[:])
+        base = psum.tile([P, HALVES, M], F32, name="base")
         for h in range(HALVES):
-            top = keep.tile([P, M], F32, name="top_%d" % h)
-            nc.vector.tensor_tensor(top[:], edge_last[h][:], best[:, h, :], ALU.max)
-            result = keep.tile([P, M], F32, name="result_%d" % h)
-            nc.vector.tensor_tensor(result[:], top[:], base[:, h, :], ALU.add)
-            nc.sync.dma_start(out_rows[h], result[:])
+            for n, part in enumerate((r_t, own_t)):
+                nc.tensor.matmul(base[:, h, :], part[:, h * P : (h + 1) * P], ident[:],
+                                 start=(n == 0), stop=(n == 1), is_transpose=True)
+
+        for g in range(G):
+            edge_product(g, 1, quantise(d1_bf[g][:], "d1_%d" % g), 0)
+
+
+        best = keep.tile([P, HALVES, M], F32, name="best", tag="d1_bf_%d" % (G - 1), align_bytes=64)
+        for h in range(HALVES):
+            nc.vector.tensor_reduce(best[:, h, :], early[h][:].rearrange("p g n -> p n g"), mybir.AxisListType.X, ALU.max)
+        top = keep.tile([P, HALVES, M], F32, name="top")
+        for h in range(HALVES):
+            nc.vector.tensor_tensor(top[:, h, :], late[h][:], best[:, h, :], ALU.max)
+        result = keep.tile([P, HALVES, M], F32, name="result")
+        for h in range(HALVES):
+            nc.vector.tensor_tensor(result[:, h, :], top[:, h, :], base[:, h, :], ALU.add)
+        nc.sync.dma_start(out.rearrange("(h p) n -> p h n", p=P), result[:])

@@ -47,16 +47,17 @@ def tile_list_edge_tm_res_kernel(tc, xT, c, w4_words, w4_scales, w8_words, w8_sc
         c_rows = c.rearrange("(a p i) j -> a p i j", a=PASSES, i=PACK)
         x_sb = [[keep.tile([P, T], F32, name="x_%d_%d" % (a, i), align_bytes=64) for i in range(PACK)] for a in range(PASSES)]
         c_sb = [keep.tile([P, PACK, G, S], F32, name="c_%d" % a) for a in range(PASSES)]
-        c_ahead = {(0, 0): [(0, 0, 1)], (0, 1): [(0, 1, 4)], (0, 3): [(1, 0, 2)], (1, 1): [(1, 2, 4)]}
+        c_ahead = {(0, 0): [(0, 0, 1)], (0, 1): [(0, 1, 4)], (0, 3): [(1, 0, 2)], (1, 2): [(1, 2, 4)]}
         w8_sb = keep.tile([P, PASSES, 4 * M], U8, name="w8_sb", align_bytes=64)
         r_sb = keep.tile([P, HALVES, M], F32, name="r_sb")
         for a in range(PASSES):
             for i in range(PACK):
-                if (a, i) == (1, 2):
+                if (a, i) == (1, 3):
                     nc.sync.dma_start(r_sb[:], r.rearrange("(h p) n -> p h n", p=P))
                     nc.sync.dma_start(w8_sb[:].bitcast(I32), w8_words.rearrange("a p n i -> p a (n i)").bitcast(I32))
                 for ca, i0, i1 in c_ahead.get((a, i), []):
-                    nc.sync.dma_start(c_sb[ca][:, i0:i1, 0, :], c_rows[ca][:, i0:i1, :])
+                    queue = nc.scalar if (a, i) == (0, 0) else nc.sync
+                    queue.dma_start(c_sb[ca][:, i0:i1, 0, :], c_rows[ca][:, i0:i1, :])
                 nc.sync.dma_start(x_sb[a][i][:], x_rows[a][i])
 
         w4_sb = keep.tile([P, PASSES, 2 * M], U8, name="w4_sb", align_bytes=64)
@@ -165,4 +166,5 @@ def tile_list_edge_tm_res_kernel(tc, xT, c, w4_words, w4_scales, w8_words, w8_sc
         result = keep.tile([P, HALVES, M], F32, name="result")
         for h in range(HALVES):
             nc.vector.tensor_tensor(result[:, h, :], top[:, h, :], base[:, h, :], ALU.add)
-        nc.sync.dma_start(out.rearrange("(h p) n -> p h n", p=P), result[:])
+            queue = nc.sync if h == 0 else nc.scalar
+            queue.dma_start(out[h * P : (h + 1) * P, :], result[:, h, :])

from contextlib import ExitStack

import concourse.mybir as mybir
from concourse.masks import make_identity

G, K, M, T, S = 4, 1024, 128, 2048, 256
FLOPS = 2 * K * M * S * (G + 1)

F32 = mybir.dt.float32
BF16 = mybir.dt.bfloat16
I32 = mybir.dt.int32
U32 = mybir.dt.uint32
U16 = mybir.dt.uint16
U8 = mybir.dt.uint8
FP8X4 = mybir.dt.float8_e4m3fn_x4
FP4X4 = mybir.dt.float4_e2m1fn_x4
ALU = mybir.AluOpType

P = 128
PACK = 4
PASSES = K // (P * PACK)
HALVES = S // P


def tile_list_edge_tm_res_kernel(tc, xT, c, w4_words, w4_scales, w8_words, w8_scales, r, offs, out):
    nc = tc.nc
    with ExitStack() as ctx:
        keep = ctx.enter_context(tc.tile_pool(name="keep", bufs=1))
        ring = ctx.enter_context(tc.tile_pool(name="ring", bufs=3))
        psum = ctx.enter_context(tc.psum_pool(name="psum", bufs=1))

        offsets = keep.tile([P, G * S // 16], U16, name="offsets")
        nc.sync.dma_start(offsets[:], offs)

        w4_sc = keep.tile([P, PASSES, M], U8, name="w4_sc", align_bytes=64)
        w8_sc = keep.tile([P, PASSES, M], U8, name="w8_sc", align_bytes=64)
        for plane, src in ((w4_sc, w4_scales), (w8_sc, w8_scales)):
            nc.gpsimd.memset(plane[:].bitcast(I32), 0)
            for q in range(4):
                nc.gpsimd.dma_start(plane[32 * q : 32 * q + 4, :, :].bitcast(I32),
                                    src[:, 4 * q : 4 * q + 4, :].rearrange("a r n -> r a n").bitcast(I32))

        ident = keep.tile([P, P], F32, name="ident")
        make_identity(nc, ident[:])

        x_rows = xT.rearrange("(a p i) t -> a i p t", a=PASSES, i=PACK)
        c_rows = c.rearrange("(a p i) j -> a p i j", a=PASSES, i=PACK)
        x_sb = [[keep.tile([P, T], F32, name="x_%d_%d" % (a, i), align_bytes=64) for i in range(PACK)] for a in range(PASSES)]
        c_sb = [keep.tile([P, PACK, G, S], F32, name="c_%d" % a) for a in range(PASSES)]
        c_ahead = {(0, 0): [(0, 0, 1)], (0, 1): [(0, 1, 4)], (0, 3): [(1, 0, 2)], (1, 2): [(1, 2, 4)]}
        w8_sb = keep.tile([P, PASSES, 4 * M], U8, name="w8_sb", align_bytes=64)
        r_sb = keep.tile([P, HALVES, M], F32, name="r_sb")
        for a in range(PASSES):
            for i in range(PACK):
                if (a, i) == (1, 3):
                    nc.sync.dma_start(r_sb[:], r.rearrange("(h p) n -> p h n", p=P))
                    nc.sync.dma_start(w8_sb[:].bitcast(I32), w8_words.rearrange("a p n i -> p a (n i)").bitcast(I32))
                for ca, i0, i1 in c_ahead.get((a, i), []):
                    queue = nc.scalar if (a, i) == (0, 0) else nc.sync
                    queue.dma_start(c_sb[ca][:, i0:i1, 0, :], c_rows[ca][:, i0:i1, :])
                nc.sync.dma_start(x_sb[a][i][:], x_rows[a][i])

        w4_sb = keep.tile([P, PASSES, 2 * M], U8, name="w4_sb", align_bytes=64)
        nc.sync.dma_start(w4_sb[:].bitcast(I32), w4_words.rearrange("a p b -> p a b").bitcast(I32))

        def interleave(grouped, planes, i0):
            count = planes.shape[1]
            if count == PACK:
                nc.scalar.copy(grouped.rearrange("p (b e) i -> p b i e", e=4),
                               planes.rearrange("p i (b e) -> p b i e", e=4))
            else:
                nc.scalar.copy(grouped[:, :, i0 : i0 + count], planes.rearrange("p i j -> p j i"))

        def quantise(grouped, name, tag=None):
            width = grouped.shape[1]
            codes = keep.tile([P, width], U32, name="codes_" + name, tag=tag or "codes_" + name, align_bytes=64)
            scales = keep.tile([P, width], U8, name="scales_" + name, align_bytes=64)
            nc.vector.quantize_mx(out=codes[:].bitcast(FP8X4), scales=scales[:],
                                  in_=grouped.rearrange("p j i -> p (j i)"))
            return codes, scales

        def product(acc, a, operand, j0, w_sb, w_dtype, w_sc, start, stop):
            codes, scales = operand
            nc.tensor.matmul_mx(out=acc, lhsT=codes[:, j0 : j0 + P].bitcast(FP8X4), lhsT_scale=scales[:, j0 : j0 + P],
                                rhs=w_sb[:, a, :].bitcast(w_dtype), rhs_scale=w_sc[:, a, :], start=start, stop=stop)

        early = [psum.tile([P, G - 1, M], F32, name="early_%d" % h) for h in range(HALVES)]
        late = [psum.tile([P, M], F32, name="late_%d" % h) for h in range(HALVES)]

        def edge_product(g, a, operand, j0):
            for h in range(HALVES):
                if g < G - 1:
                    product(early[h][:, g, :], a, operand, j0 + h * P, w4_sb, FP4X4, w4_sc,
                            start=(a == 0 and g == 0), stop=(a == PASSES - 1 and g == G - 2))
                else:
                    product(late[h][:], a, operand, j0 + h * P, w4_sb, FP4X4, w4_sc,
                            start=(a == 0), stop=(a == PASSES - 1))

        def wide_pair(a, i0, targets):
            diff = keep.tile([P, 2, G, S], F32, name="diff_%d_%d" % (a, i0))
            for e in range(2):
                nc.vector.tensor_tensor(diff[:, e].rearrange("p g j -> p (g j)"), x_sb[a][i0 + e][:].indirect(offsets[:]),
                                        c_sb[a][:, i0 + e].rearrange("p g j -> p (g j)"), ALU.subtract)
            for g in range(G):
                interleave(targets[g], diff[:, :, g, :], i0)

        for a, planes in ((0, PACK), (1, 2)):
            for i in range(planes):
                nc.scalar.copy(c_sb[a][:, i, 1:G, :], c_sb[a][:, i, 0:1, :].to_broadcast([P, G - 1, S]))
        c_bf = [keep.tile([P, S, PACK], BF16, name="c_bf_%d" % a, align_bytes=64) for a in range(PASSES)]
        for a in range(PASSES):
            interleave(c_bf[a][:], c_sb[a][:, :, 0, :], 0)

        d0_bf = [keep.tile([P, 2 * S, PACK], BF16, name="d0_bf_%d" % gp, align_bytes=64) for gp in range(2)]
        d1_bf = [keep.tile([P, S, PACK], BF16, name="d1_bf_%d" % g, align_bytes=64) for g in range(G)]
        d0_of = [d0_bf[g // 2][:, (g % 2) * S : (g % 2 + 1) * S, :] for g in range(G)]
        wide_pair(0, 0, d0_of)
        wide_pair(0, 2, d0_of)
        wide_pair(1, 0, [tile[:] for tile in d1_bf])
        c_q = [quantise(c_bf[0][:], "c_0")]
        for gp in range(2):
            d0_q = quantise(d0_bf[gp][:], "d0_%d" % gp, tag="x_1_%d" % gp)
            for gg in range(2):
                edge_product(2 * gp + gg, 0, d0_q, gg * S)

        for g in range(G):
            width = S if g < G - 1 else P
            diff = ring.tile([P, S // width, 2, width], F32, name="diff_last", tag="diff_last")
            for piece in range(S // width):
                j0 = piece * width
                first = (g * S + j0) // 16
                for e in range(2):
                    nc.vector.tensor_tensor(diff[:, piece, e, :],
                                            x_sb[1][2 + e][:].indirect(offsets[:, first : first + width // 16]),
                                            c_sb[1][:, 2 + e, 0, j0 : j0 + width], ALU.subtract)
                interleave(d1_bf[g][:, j0 : j0 + width, :], diff[:, piece], 2)
        c_q.append(quantise(c_bf[1][:], "c_1", tag="d0_bf_1"))
        r_turned = psum.tile([P, S], F32, name="r_turned")
        for h in range(HALVES):
            nc.tensor.transpose(r_turned[:, h * P : (h + 1) * P], r_sb[:, h, :], ident[:])
        r_t = keep.tile([P, S], F32, name="r_t")
        nc.scalar.copy(r_t[:], r_turned[:])
        own = psum.tile([P, S], F32, name="own")
        for a in range(PASSES):
            nc.tensor.matmul_mx(out=own[:], lhsT=w8_sb[:, a, :].bitcast(FP8X4), lhsT_scale=w8_sc[:, a, :],
                                rhs=c_q[a][0][:].bitcast(FP8X4), rhs_scale=c_q[a][1][:],
                                start=(a == 0), stop=(a == PASSES - 1))
        own_t = keep.tile([P, S], F32, name="own_t")
        nc.scalar.copy(own_t[:], own[:])
        base = psum.tile([P, HALVES, M], F32, name="base")
        for h in range(HALVES):
            for n, part in enumerate((r_t, own_t)):
                nc.tensor.matmul(base[:, h, :], part[:, h * P : (h + 1) * P], ident[:],
                                 start=(n == 0), stop=(n == 1), is_transpose=True)

        for g in range(G):
            edge_product(g, 1, quantise(d1_bf[g][:], "d1_%d" % g), 0)


        best = keep.tile([P, HALVES, M], F32, name="best", tag="d1_bf_%d" % (G - 1), align_bytes=64)
        for h in range(HALVES):
            nc.vector.tensor_reduce(best[:, h, :], early[h][:].rearrange("p g n -> p n g"), mybir.AxisListType.X, ALU.max)
        top = keep.tile([P, HALVES, M], F32, name="top")
        for h in range(HALVES):
            nc.vector.tensor_tensor(top[:, h, :], late[h][:], best[:, h, :], ALU.max)
        result = keep.tile([P, HALVES, M], F32, name="result")
        for h in range(HALVES):
            nc.vector.tensor_tensor(result[:, h, :], top[:, h, :], base[:, h, :], ALU.add)
            queue = nc.sync if h == 0 else nc.scalar
            queue.dma_start(out[h * P : (h + 1) * P, :], result[:, h, :])
